import numpy as np
import ml_dtypes


def mxq(x, axis, fmt="e4m3"):
    dtype, down = {"e4m3": (ml_dtypes.float8_e4m3fn, 7), "e5m2": (ml_dtypes.float8_e5m2, 14)}[fmt]
    v = np.moveaxis(np.asarray(x, np.float32).astype(ml_dtypes.bfloat16).astype(np.float64), axis, -1)
    blocks = v.reshape(v.shape[:-1] + (-1, 32))
    amax = np.abs(blocks).max(-1, keepdims=True)
    byte = np.maximum(np.where(amax > 0, np.frexp(amax)[1] - 1 + 127, 0) - down, 1)
    scale = np.exp2(byte - 127.0)
    codes = (blocks / scale).astype(np.float32).astype(dtype).astype(np.float64)
    return np.moveaxis((codes * scale).reshape(v.shape), -1, axis)


WIDE = False


def mx_kscale(k):
    if not WIDE:
        return np.ones(k)
    levels = np.array([10, -10, 5, -5, 0])
    if k % 512:
        return np.exp2(np.random.permutation(np.resize(levels, k // 32))).repeat(32)
    a = np.empty((k // 512, 16))
    for p in range(k // 512):
        a[p, :8] = np.random.permutation(np.resize(levels, 8))
        for g in range(8):
            far = levels[np.abs(levels - a[p, g]) >= 10]
            a[p, g + 8] = far[np.random.randint(len(far))]
    return np.exp2(a.ravel()).repeat(32)


BF16 = ml_dtypes.bfloat16


def bf(x):
    return np.asarray(x, np.float32).astype(BF16)


def f64(x):
    return np.asarray(x).astype(np.float64)

def planes(Y):
    n, m = Y.shape
    b = f64(bf(Y)).reshape(n // 32, 32, m)
    amax = np.abs(b).max(1)
    byte = np.clip(np.where(amax > 0, np.frexp(amax)[1] - 1 + 127 - 7, 1), 1, 254)
    codes = (b * np.exp2(127.0 - byte)[:, None, :]).reshape(n, m).astype(np.float32).astype(ml_dtypes.float8_e4m3fn).view(np.uint8)
    words = codes.reshape(n // 512, 128, 4, m).transpose(0, 1, 3, 2)
    return np.ascontiguousarray(words), np.ascontiguousarray(byte.astype(np.uint8).reshape(n // 512, 16, m))


H, T, DK, DV = 4, 1024, 1024, 512

def setup_inputs():
    s = mx_kscale(T)
    gaps = 3.0 * np.random.rand(H, T) / T
    left = np.exp(np.cumsum(gaps, axis=1) - np.sum(gaps, axis=1, keepdims=True))
    write = left / np.sqrt(T) * s
    keys = np.random.randn(H, T, DK)
    values = np.random.randn(H, T, DV) / s[:, None]
    gain = np.exp(0.8 * np.random.randn(H, DK))
    keep = np.exp(-np.random.rand(H, DK))
    state = np.random.randn(H, DK, DV) * gain[:, :, None]
    return {"keys": bf(keys), "values": bf(values), "write": bf(write),
            "gain": bf(gain), "keep": bf(keep), "state": bf(state)}

def reference(keys, values, write, gain, keep, state):
    x = f64(keys)
    feat = np.exp(np.minimum(x, 0.0)) + np.maximum(x, 0.0)
    feat = feat * f64(write)[:, :, None]
    fq = mxq(feat, 1, "e4m3")
    vq = mxq(f64(values), 1, "e4m3")
    upd = fq.swapaxes(1, 2) @ vq
    y = f64(keep)[:, :, None] * f64(state) + f64(gain)[:, :, None] * upd
    Y = y.transpose(1, 0, 2).reshape(DK, H * DV)
    words, scales = planes(Y)
    return y, words, scales

@@ -1,0 +1,347 @@
+from contextlib import ExitStack
+
+import concourse.mybir as mybir
+
+H, T, DK, DV = 4, 1024, 1024, 512
+FLOPS = 2 * H * T * DK * DV
+
+F32 = mybir.dt.float32
+BF16 = mybir.dt.bfloat16
+I32 = mybir.dt.int32
+U32 = mybir.dt.uint32
+U8 = mybir.dt.uint8
+FP8X4 = mybir.dt.float8_e4m3fn_x4
+ALU = mybir.AluOpType
+ACT = mybir.ActivationFunctionType
+
+P = 128
+PACK = 4
+GROUP = P * PACK
+COLS = PACK * GROUP
+TOKEN_GROUPS = T // GROUP
+CHANNEL_GROUPS = DK // GROUP
+BLOCKS = H * CHANNEL_GROUPS
+STEPS = BLOCKS * TOKEN_GROUPS
+VALUE_TILES = H * TOKEN_GROUPS
+RUN = 4
+
+LN_LOW, LN_HIGH = 2.0 ** -64, 2.0 ** 64
+SMALLEST_NORMAL = 2.0 ** -126
+
+
+SHARE_EVEN = 44
+SHARE_ODD = 44
+SHARE_HEAD = 16
+SHARE_14 = 88
+SHARE_LAST = 44
+TAIL_SPLIT = 160
+GPSIMD_SLOTS = (3, 0, 1)
+
+
+def scalar_share(step):
+    if step < 2:
+        return SHARE_HEAD
+    return {14: SHARE_14, 15: SHARE_LAST}.get(step, SHARE_ODD if step % 2 else SHARE_EVEN)
+
+
+def tile_linear_attention_state_handoff_g2_kernel(
+    tc, keys, values, write, gain, keep, state, out_0, out_1, out_2
+):
+    nc = tc.nc
+    with ExitStack() as ctx:
+        sbuf = ctx.enter_context(tc.tile_pool(name="sbuf", bufs=1))
+        psum = ctx.enter_context(tc.psum_pool(name="psum", bufs=1))
+        ctx.enter_context(tc.manual_schedule())
+
+        def ring(name, count, shape, dtype):
+            return [sbuf.tile(shape, dtype, name="%s%d" % (name, i), align_bytes=64) for i in range(count)]
+
+        def one(name, shape, dtype):
+            return ring(name, 1, shape, dtype)[0]
+
+        keys_raw = ring("keys_raw", 6, [P, COLS], BF16)
+        values_raw = ring("values_raw", 3, [P, COLS], BF16)
+        state_raw = ring("state_raw", 3, [P, COLS], BF16)
+        negative = ring("negative", 3, [P, COLS], BF16)
+        exp_branch = ring("exp_branch", 3, [P, COLS], BF16)
+        linear_branch = ring("linear_branch", 3, [P, COLS], BF16)
+        feat = ring("feat", 2, [P, COLS], BF16)
+        feat_words = ring("feat_words", 2, [P, COLS], BF16)
+        feat_codes = ring("feat_codes", 2, [P, GROUP], U32)
+        feat_scales = ring("feat_scales", 2, [P, GROUP], U8)
+        values_signed = ring("values_signed", 2, [P, COLS], BF16)
+        values_words = ring("values_words", 2, [P, COLS], BF16)
+        values_codes = ring("values_codes", 4, [P, DV], U32)
+        values_scales = ring("values_scales", 4, [P, DV], U8)
+        kept = ring("kept", 4, [P, DV], F32)
+        y = ring("y", 3, [P, COLS], F32)
+        y_words = ring("y_words", 2, [P, COLS], BF16)
+        y_codes = ring("y_codes", 2, [P, DV], U32)
+        y_scales = ring("y_scales", CHANNEL_GROUPS, [P, H * DV], U8)
+        upd = [psum.tile([P, DV], F32, name="upd%d" % i) for i in range(2 * PACK)]
+
+        width = VALUE_TILES * PACK
+        write_sb = one("write_sb", [P, width], BF16)
+        gain_sb = one("gain_sb", [P, width], BF16)
+        keep_sb = one("keep_sb", [P, width], BF16)
+        keep_f32 = one("keep_f32", [P, width], F32)
+        sign_twice = one("sign_twice", [P, width], F32)
+        sign = one("sign", [P, width], F32)
+        size = one("size", [P, width], F32)
+        size_low = one("size_low", [P, width], F32)
+        factors = one("factors", [P, 3 * width], F32)
+        ln_factors = one("ln_factors", [P, 3 * width], F32)
+        ln_size = one("ln_size", [P, width], F32)
+
+        def slot(tile, j):
+            return tile[:, j * GROUP : (j + 1) * GROUP]
+
+        def column(tile, index, j):
+            return tile[:, index * PACK + j : index * PACK + j + 1]
+
+        def rows_of(tensor, head, group):
+            return tensor[head, group * GROUP : (group + 1) * GROUP, :].rearrange("(p j) c -> p j c", j=PACK)
+
+        def by_slot(tile):
+            return tile[:].rearrange("p (j c) -> p j c", j=PACK)
+
+        def value_tile(step):
+            return step // (CHANNEL_GROUPS * TOKEN_GROUPS) * TOKEN_GROUPS + step % TOKEN_GROUPS
+
+        def load_vector(tile, vector):
+            nc.sync.dma_start(
+                out=tile[:].rearrange("p (k j) -> p k j", j=PACK),
+                in_=vector.rearrange("h (g p j) -> p (h g) j", p=P, j=PACK),
+            )
+
+        def load_keys(step):
+            head, channel_group = divmod(step // TOKEN_GROUPS, CHANNEL_GROUPS)
+            rows = rows_of(keys, head, step % TOKEN_GROUPS)
+            nc.sync.dma_start(
+                out=by_slot(keys_raw[step % len(keys_raw)]),
+                in_=rows[:, :, channel_group * GROUP : (channel_group + 1) * GROUP],
+            )
+
+        def load_values(k):
+            nc.sync.dma_start(out=by_slot(values_raw[k % len(values_raw)]), in_=rows_of(values, *divmod(k, TOKEN_GROUPS)))
+
+        def load_state(block):
+            nc.sync.dma_start(out=by_slot(state_raw[block % len(state_raw)]), in_=rows_of(state, *divmod(block, CHANNEL_GROUPS)))
+
+        def prepare_write():
+            nc.vector.scalar_tensor_tensor(size[:], write_sb[:], -1.0, write_sb[:], ALU.mult, ALU.max)
+            nc.vector.tensor_scalar(sign_twice[:], write_sb[:], 0.0, 2.0, ALU.is_ge, ALU.mult)
+            nc.vector.tensor_scalar(size_low[:], size[:], SMALLEST_NORMAL, LN_LOW, ALU.max, ALU.min)
+            nc.vector.tensor_scalar(factors[:, 0:width], size[:], LN_LOW, LN_HIGH, ALU.max, ALU.min)
+            nc.vector.tensor_scalar(factors[:, width : 2 * width], size[:], LN_HIGH, LN_LOW, ALU.max, ALU.mult)
+            nc.vector.tensor_scalar(factors[:, 2 * width :], size_low[:], LN_HIGH, None, ALU.mult)
+            nc.vector.tensor_scalar(sign[:], sign_twice[:], -1.0, None, ALU.add)
+            nc.scalar.activation(ln_factors[:], factors[:], ACT.Ln)
+
+        def sum_logs():
+            nc.vector.tensor_reduce(
+                ln_size[:], ln_factors[:].rearrange("p (r c) -> p c r", r=3), mybir.AxisListType.X, ALU.add
+            )
+
+        def negative_part(step):
+            nc.vector.tensor_scalar(negative[step % 3][:], keys_raw[step % len(keys_raw)][:], 0.0, None, ALU.min)
+
+        def linear(step):
+            for j in range(PACK):
+                nc.vector.tensor_scalar(
+                    slot(linear_branch[step % 3], j), slot(keys_raw[step % len(keys_raw)], j),
+                    1.0, column(size, value_tile(step), j), ALU.add, ALU.mult,
+                )
+
+        def exponential(step):
+            for j in range(PACK):
+                nc.scalar.activation(
+                    slot(exp_branch[step % 3], j), slot(negative[step % 3], j), ACT.Exp,
+                    bias=column(ln_size, value_tile(step), j),
+                )
+
+        def combine(step):
+            nc.vector.tensor_tensor(feat[step % 2][:], exp_branch[step % 3][:], linear_branch[step % 3][:], ALU.max)
+
+        def interleave_feat(copy, step, start, stop):
+            if start == stop:
+                return
+            source = feat[step % 2][:].rearrange("p (j m t) -> p m j t", j=PACK, t=PACK)
+            target = feat_words[step % 2][:].rearrange("p (t m j) -> p m j t", j=PACK, t=PACK)
+            copy(target[:, start:stop], source[:, start:stop])
+
+        def interleave(copy, target, source):
+            copy(
+                target.rearrange("p (c i j) -> p c j i", i=RUN, j=PACK),
+                source.rearrange("p j (c i) -> p c j i", i=RUN),
+            )
+
+        def quantize(codes, scales, words):
+            nc.vector.quantize_mx(out=codes.bitcast(FP8X4), scales=scales, in_=words)
+
+        def multiply(step):
+            block, token_group = divmod(step, TOKEN_GROUPS)
+            k = value_tile(step) % len(values_codes)
+            for t in range(PACK):
+                cols = slice(t * P, (t + 1) * P)
+                nc.tensor.matmul_mx(
+                    out=upd[block % 2 * PACK + t][:],
+                    lhsT=feat_codes[step % 2][:, cols].bitcast(FP8X4),
+                    lhsT_scale=feat_scales[step % 2][:, cols],
+                    rhs=values_codes[k][:].bitcast(FP8X4),
+                    rhs_scale=values_scales[k][:],
+                    start=token_group == 0,
+                    stop=token_group == TOKEN_GROUPS - 1,
+                )
+
+        def quantize_feat(step):
+            quantize(feat_codes[step % 2][:], feat_scales[step % 2][:], feat_words[step % 2][:])
+            multiply(step)
+
+        def sign_values(k):
+            for j in range(PACK):
+                nc.vector.tensor_scalar(
+                    slot(values_signed[k % 2], j), slot(values_raw[k % len(values_raw)], j),
+                    column(sign, k, j), None, ALU.mult,
+                )
+
+        def interleave_values(copy, k):
+            interleave(copy, values_words[k % 2][:], by_slot(values_signed[k % 2]))
+
+        def quantize_values(k):
+            quantize(values_codes[k % len(values_codes)][:], values_scales[k % len(values_scales)][:], values_words[k % 2][:])
+
+        def kept_tile(block, t):
+            if block > 0 and t == GPSIMD_SLOTS[0]:
+                return linear_branch[2 * block % 3][:].bitcast(F32)[:, 0:DV]
+            return kept[t][:]
+
+        def keep_state_scalar(block, t):
+            nc.scalar.activation(
+                kept_tile(block, t), slot(state_raw[block % len(state_raw)], t), ACT.Copy, scale=column(keep_f32, block, t)
+            )
+
+        def keep_state(engine, block, t):
+            engine.tensor_scalar(
+                kept_tile(block, t), slot(state_raw[block % len(state_raw)], t), column(keep_f32, block, t), 0.0,
+                ALU.mult, ALU.add,
+            )
+
+        def new_state(block, t, cols):
+            nc.vector.scalar_tensor_tensor(
+                slot(y[block % len(y)], t)[:, cols], upd[block % 2 * PACK + t][:, cols], column(gain_sb, block, t),
+                kept_tile(block, t)[:, cols], ALU.mult, ALU.add,
+            )
+
+        def store_state(block, cols):
+            nc.sync.dma_start(
+                out=rows_of(out_0, *divmod(block, CHANNEL_GROUPS))[:, :, cols], in_=by_slot(y[block % len(y)])[:, :, cols]
+            )
+
+        def interleave_state(copy, block, start, stop):
+            interleave(
+                copy, y_words[block % 2][:, PACK * start : PACK * stop], by_slot(y[block % len(y)])[:, :, start:stop]
+            )
+
+        def quantize_state(block, start, stop):
+            head, channel_group = divmod(block, CHANNEL_GROUPS)
+            cols = slice(head * DV + start, head * DV + stop)
+            codes = y_codes[block % 2][:, start:stop]
+            quantize(codes, y_scales[channel_group][:, cols], y_words[block % 2][:, PACK * start : PACK * stop])
+            nc.sync.dma_start(
+                out=out_1[channel_group, :, cols, :].rearrange("p m t -> p (m t)").bitcast(I32), in_=codes.bitcast(I32)
+            )
+
+        def store_scales(block, queues):
+            head, channel_group = divmod(block, CHANNEL_GROUPS)
+            cols = slice(head * DV, (head + 1) * DV)
+            for quadrant in range(4):
+                queues[quadrant % len(queues)].dma_start(
+                    out=out_2[channel_group, 4 * quadrant : 4 * quadrant + 4, cols].bitcast(I32),
+                    in_=y_scales[channel_group][32 * quadrant : 32 * quadrant + 4, cols].bitcast(I32),
+                )
+
+        load_vector(write_sb, write)
+        load_keys(0)
+        load_values(0)
+        load_keys(1)
+        load_keys(2)
+        load_values(1)
+        load_vector(keep_sb, keep)
+        load_state(0)
+        load_keys(3)
+        load_values(2)
+        load_vector(gain_sb, gain)
+        load_state(1)
+        load_keys(4)
+
+        prepare_write()
+        negative_part(0)
+        sum_logs()
+        linear(0)
+        exponential(0)
+        sign_values(0)
+        negative_part(1)
+        exponential(1)
+        interleave_values(nc.vector.tensor_copy, 0)
+
+        whole = slice(0, DV)
+        last = BLOCKS - 1
+        for step in range(STEPS):
+            pair, odd = divmod(step, 2)
+            split = P - scalar_share(step)
+            if step + 5 < STEPS:
+                load_keys(step + 5)
+            if step + 2 < STEPS:
+                negative_part(step + 2)
+                exponential(step + 2)
+            combine(step)
+            interleave_feat(nc.scalar.copy, step, split, P)
+            if step == 0:
+                sign_values(1)
+            if odd and pair + 2 < VALUE_TILES:
+                sign_values(pair + 2)
+                if pair + 3 < VALUE_TILES:
+                    load_values(pair + 3)
+            if not odd and pair >= 1:
+                for t in range(PACK):
+                    new_state(pair - 1, t, whole)
+                store_state(pair - 1, whole)
+                for t in GPSIMD_SLOTS:
+                    keep_state(nc.gpsimd, pair, t)
+            if odd and pair >= 2:
+                quantize_state(pair - 2, 0, DV)
+                store_scales(pair - 2, [nc.sync])
+            interleave_feat(nc.vector.tensor_copy, step, 0, split)
+            if step + 1 < STEPS:
+                linear(step + 1)
+            if step == 0:
+                quantize_values(0)
+                nc.vector.tensor_copy(keep_f32[:], keep_sb[:])
+            if odd and pair + 1 < VALUE_TILES:
+                quantize_values(pair + 1)
+            quantize_feat(step)
+            if not odd and pair < last:
+                interleave_values(nc.scalar.copy, pair + 1)
+            if step == min(2 * pair + 1, STEPS - 2):
+                for t in range(PACK):
+                    if t not in GPSIMD_SLOTS or pair == 0:
+                        keep_state_scalar(pair, t)
+                if pair + 2 < BLOCKS:
+                    load_state(pair + 2)
+                if pair >= 1:
+                    interleave_state(nc.scalar.copy, pair - 1, 0, DV)
+
+        quantize_state(last - 1, 0, DV)
+        store_scales(last - 1, [nc.sync])
+        half = DV // 2
+        for cols in (slice(0, half), slice(half, DV)):
+            for t in range(PACK):
+                new_state(last, t, cols)
+            store_state(last, cols)
+        interleave_state(nc.scalar.copy, last, 0, half)
+        interleave_state(nc.scalar.copy, last, half + TAIL_SPLIT, DV)
+        interleave_state(nc.vector.tensor_copy, last, half, half + TAIL_SPLIT)
+        quantize_state(last, 0, half)
+        quantize_state(last, half, DV)
+        store_scales(last, [nc.scalar, nc.sync])

@@ -23,18 +23,18 @@ CHANNEL_GROUPS = DK // GROUP
 BLOCKS = H * CHANNEL_GROUPS
 STEPS = BLOCKS * TOKEN_GROUPS
 VALUE_TILES = H * TOKEN_GROUPS
-RUN = 4
+RUN = 2
 
 LN_LOW, LN_HIGH = 2.0 ** -64, 2.0 ** 64
 SMALLEST_NORMAL = 2.0 ** -126
 
 
-SHARE_EVEN = 44
+SHARE_EVEN = 48
 SHARE_ODD = 44
 SHARE_HEAD = 16
-SHARE_14 = 88
+SHARE_14 = 128
 SHARE_LAST = 44
-TAIL_SPLIT = 160
+TAIL_SPLIT = 144
 GPSIMD_SLOTS = (3, 0, 1)
 
 
@@ -77,7 +77,7 @@ def tile_linear_attention_state_handoff_g2_kernel(
         y = ring("y", 3, [P, COLS], F32)
         y_words = ring("y_words", 2, [P, COLS], BF16)
         y_codes = ring("y_codes", 2, [P, DV], U32)
-        y_scales = ring("y_scales", CHANNEL_GROUPS, [P, H * DV], U8)
+        y_scales = one("y_scales", [P, H * DV], U8)
         upd = [psum.tile([P, DV], F32, name="upd%d" % i) for i in range(2 * PACK)]
 
         width = VALUE_TILES * PACK
@@ -166,9 +166,9 @@ def tile_linear_attention_state_handoff_g2_kernel(
         def interleave_feat(copy, step, start, stop):
             if start == stop:
                 return
-            source = feat[step % 2][:].rearrange("p (j m t) -> p m j t", j=PACK, t=PACK)
-            target = feat_words[step % 2][:].rearrange("p (t m j) -> p m j t", j=PACK, t=PACK)
-            copy(target[:, start:stop], source[:, start:stop])
+            source = feat[step % 2][:].rearrange("p (j m i t) -> p m t j i", j=PACK, i=RUN, t=PACK)
+            target = feat_words[step % 2][:].rearrange("p (t m i j) -> p m t j i", j=PACK, i=RUN, t=PACK)
+            copy(target[:, start // RUN : stop // RUN], source[:, start // RUN : stop // RUN])
 
         def interleave(copy, target, source):
             copy(
@@ -179,20 +179,30 @@ def tile_linear_attention_state_handoff_g2_kernel(
         def quantize(codes, scales, words):
             nc.vector.quantize_mx(out=codes.bitcast(FP8X4), scales=scales, in_=words)
 
+        def column_parts(block):
+            if block < BLOCKS - 1:
+                return [slice(0, DV)]
+            return [slice(0, DV // 2), slice(DV // 2, DV)]
+
+        def sums(block, t, part):
+            cols = column_parts(block)[part]
+            return upd[(block + part) % 2 * PACK + t][:, 0 : cols.stop - cols.start]
+
         def multiply(step):
             block, token_group = divmod(step, TOKEN_GROUPS)
             k = value_tile(step) % len(values_codes)
-            for t in range(PACK):
-                cols = slice(t * P, (t + 1) * P)
-                nc.tensor.matmul_mx(
-                    out=upd[block % 2 * PACK + t][:],
-                    lhsT=feat_codes[step % 2][:, cols].bitcast(FP8X4),
-                    lhsT_scale=feat_scales[step % 2][:, cols],
-                    rhs=values_codes[k][:].bitcast(FP8X4),
-                    rhs_scale=values_scales[k][:],
-                    start=token_group == 0,
-                    stop=token_group == TOKEN_GROUPS - 1,
-                )
+            for part, cols in enumerate(column_parts(block)):
+                for t in range(PACK):
+                    channels = slice(t * P, (t + 1) * P)
+                    nc.tensor.matmul_mx(
+                        out=sums(block, t, part),
+                        lhsT=feat_codes[step % 2][:, channels].bitcast(FP8X4),
+                        lhsT_scale=feat_scales[step % 2][:, channels],
+                        rhs=values_codes[k][:, cols].bitcast(FP8X4),
+                        rhs_scale=values_scales[k][:, cols],
+                        start=token_group == 0,
+                        stop=token_group == TOKEN_GROUPS - 1,
+                    )
 
         def quantize_feat(step):
             quantize(feat_codes[step % 2][:], feat_scales[step % 2][:], feat_words[step % 2][:])
@@ -227,16 +237,18 @@ def tile_linear_attention_state_handoff_g2_kernel(
                 ALU.mult, ALU.add,
             )
 
-        def new_state(block, t, cols):
-            nc.vector.scalar_tensor_tensor(
-                slot(y[block % len(y)], t)[:, cols], upd[block % 2 * PACK + t][:, cols], column(gain_sb, block, t),
-                kept_tile(block, t)[:, cols], ALU.mult, ALU.add,
-            )
-
-        def store_state(block, cols):
-            nc.sync.dma_start(
-                out=rows_of(out_0, *divmod(block, CHANNEL_GROUPS))[:, :, cols], in_=by_slot(y[block % len(y)])[:, :, cols]
-            )
+        def new_state(block, part):
+            cols = column_parts(block)[part]
+            for t in range(PACK):
+                nc.vector.scalar_tensor_tensor(
+                    slot(y[block % len(y)], t)[:, cols], sums(block, t, part), column(gain_sb, block, t),
+                    kept_tile(block, t)[:, cols], ALU.mult, ALU.add,
+                )
+                if t % 2 == 1:
+                    nc.sync.dma_start(
+                        out=rows_of(out_0, *divmod(block, CHANNEL_GROUPS))[:, t - 1 : t + 1, cols],
+                        in_=by_slot(y[block % len(y)])[:, t - 1 : t + 1, cols],
+                    )
 
         def interleave_state(copy, block, start, stop):
             interleave(
@@ -247,18 +259,17 @@ def tile_linear_attention_state_handoff_g2_kernel(
             head, channel_group = divmod(block, CHANNEL_GROUPS)
             cols = slice(head * DV + start, head * DV + stop)
             codes = y_codes[block % 2][:, start:stop]
-            quantize(codes, y_scales[channel_group][:, cols], y_words[block % 2][:, PACK * start : PACK * stop])
+            quantize(codes, y_scales[4 * channel_group :, cols], y_words[block % 2][:, PACK * start : PACK * stop])
             nc.sync.dma_start(
                 out=out_1[channel_group, :, cols, :].rearrange("p m t -> p (m t)").bitcast(I32), in_=codes.bitcast(I32)
             )
 
-        def store_scales(block, queues):
-            head, channel_group = divmod(block, CHANNEL_GROUPS)
+        def store_scales(head, queues):
             cols = slice(head * DV, (head + 1) * DV)
             for quadrant in range(4):
                 queues[quadrant % len(queues)].dma_start(
-                    out=out_2[channel_group, 4 * quadrant : 4 * quadrant + 4, cols].bitcast(I32),
-                    in_=y_scales[channel_group][32 * quadrant : 32 * quadrant + 4, cols].bitcast(I32),
+                    out=out_2[:, 4 * quadrant : 4 * quadrant + 4, cols].bitcast(I32),
+                    in_=y_scales[32 * quadrant : 32 * quadrant + 4 * CHANNEL_GROUPS, cols].bitcast(I32),
                 )
 
         load_vector(write_sb, write)
@@ -285,7 +296,6 @@ def tile_linear_attention_state_handoff_g2_kernel(
         exponential(1)
         interleave_values(nc.vector.tensor_copy, 0)
 
-        whole = slice(0, DV)
         last = BLOCKS - 1
         for step in range(STEPS):
             pair, odd = divmod(step, 2)
@@ -304,14 +314,13 @@ def tile_linear_attention_state_handoff_g2_kernel(
                 if pair + 3 < VALUE_TILES:
                     load_values(pair + 3)
             if not odd and pair >= 1:
-                for t in range(PACK):
-                    new_state(pair - 1, t, whole)
-                store_state(pair - 1, whole)
+                new_state(pair - 1, 0)
                 for t in GPSIMD_SLOTS:
                     keep_state(nc.gpsimd, pair, t)
             if odd and pair >= 2:
                 quantize_state(pair - 2, 0, DV)
-                store_scales(pair - 2, [nc.sync])
+                if pair % 2 == 1:
+                    store_scales(pair // 2 - 1, [nc.sync])
             interleave_feat(nc.vector.tensor_copy, step, 0, split)
             if step + 1 < STEPS:
                 linear(step + 1)
@@ -323,25 +332,24 @@ def tile_linear_attention_state_handoff_g2_kernel(
             quantize_feat(step)
             if not odd and pair < last:
                 interleave_values(nc.scalar.copy, pair + 1)
-            if step == min(2 * pair + 1, STEPS - 2):
+            if not odd and pair == last:
+                interleave_state(nc.scalar.copy, last - 1, 0, DV)
+            if odd:
                 for t in range(PACK):
                     if t not in GPSIMD_SLOTS or pair == 0:
                         keep_state_scalar(pair, t)
                 if pair + 2 < BLOCKS:
                     load_state(pair + 2)
-                if pair >= 1:
-                    interleave_state(nc.scalar.copy, pair - 1, 0, DV)
+            if odd and 1 <= pair < last:
+                interleave_state(nc.scalar.copy, pair - 1, 0, DV)
 
-        quantize_state(last - 1, 0, DV)
-        store_scales(last - 1, [nc.sync])
         half = DV // 2
-        for cols in (slice(0, half), slice(half, DV)):
-            for t in range(PACK):
-                new_state(last, t, cols)
-            store_state(last, cols)
+        quantize_state(last - 1, 0, DV)
+        new_state(last, 0)
+        new_state(last, 1)
         interleave_state(nc.scalar.copy, last, 0, half)
         interleave_state(nc.scalar.copy, last, half + TAIL_SPLIT, DV)
-        interleave_state(nc.vector.tensor_copy, last, half, half + TAIL_SPLIT)
         quantize_state(last, 0, half)
+        interleave_state(nc.vector.tensor_copy, last, half, half + TAIL_SPLIT)
         quantize_state(last, half, DV)
-        store_scales(last, [nc.scalar, nc.sync])
+        store_scales(H - 1, [nc.scalar, nc.sync])

@@ -35,7 +35,8 @@ SHARE_HEAD = 16
 SHARE_14 = 128
 SHARE_LAST = 44
 TAIL_SPLIT = 144
-GPSIMD_SLOTS = (3, 0, 1)
+GPSIMD_SLOTS = (3, 0)
+VECTOR_SLOTS = (1,)
 
 
 def scalar_share(step):
@@ -317,6 +318,9 @@ def tile_linear_attention_state_handoff_g2_kernel(
                 new_state(pair - 1, 0)
                 for t in GPSIMD_SLOTS:
                     keep_state(nc.gpsimd, pair, t)
+            if odd and pair >= 1:
+                for t in VECTOR_SLOTS:
+                    keep_state(nc.vector, pair, t)
             if odd and pair >= 2:
                 quantize_state(pair - 2, 0, DV)
                 if pair % 2 == 1:
@@ -336,7 +340,7 @@ def tile_linear_attention_state_handoff_g2_kernel(
                 interleave_state(nc.scalar.copy, last - 1, 0, DV)
             if odd:
                 for t in range(PACK):
-                    if t not in GPSIMD_SLOTS or pair == 0:
+                    if t not in GPSIMD_SLOTS + VECTOR_SLOTS or pair == 0:
                         keep_state_scalar(pair, t)
                 if pair + 2 < BLOCKS:
                     load_state(pair + 2)

from contextlib import ExitStack

import concourse.mybir as mybir

H, T, DK, DV = 4, 1024, 1024, 512
FLOPS = 2 * H * T * DK * DV

F32 = mybir.dt.float32
BF16 = mybir.dt.bfloat16
I32 = mybir.dt.int32
U32 = mybir.dt.uint32
U8 = mybir.dt.uint8
FP8X4 = mybir.dt.float8_e4m3fn_x4
ALU = mybir.AluOpType
ACT = mybir.ActivationFunctionType

P = 128
PACK = 4
GROUP = P * PACK
COLS = PACK * GROUP
TOKEN_GROUPS = T // GROUP
CHANNEL_GROUPS = DK // GROUP
BLOCKS = H * CHANNEL_GROUPS
STEPS = BLOCKS * TOKEN_GROUPS
VALUE_TILES = H * TOKEN_GROUPS
RUN = 2

LN_LOW, LN_HIGH = 2.0 ** -64, 2.0 ** 64
SMALLEST_NORMAL = 2.0 ** -126


SHARE_EVEN = 48
SHARE_ODD = 44
SHARE_HEAD = 16
SHARE_14 = 128
SHARE_LAST = 44
TAIL_SPLIT = 144
GPSIMD_SLOTS = (3, 0)
VECTOR_SLOTS = (1,)


def scalar_share(step):
    if step < 2:
        return SHARE_HEAD
    return {14: SHARE_14, 15: SHARE_LAST}.get(step, SHARE_ODD if step % 2 else SHARE_EVEN)


def tile_linear_attention_state_handoff_g2_kernel(
    tc, keys, values, write, gain, keep, state, out_0, out_1, out_2
):
    nc = tc.nc
    with ExitStack() as ctx:
        sbuf = ctx.enter_context(tc.tile_pool(name="sbuf", bufs=1))
        psum = ctx.enter_context(tc.psum_pool(name="psum", bufs=1))
        ctx.enter_context(tc.manual_schedule())

        def ring(name, count, shape, dtype):
            return [sbuf.tile(shape, dtype, name="%s%d" % (name, i), align_bytes=64) for i in range(count)]

        def one(name, shape, dtype):
            return ring(name, 1, shape, dtype)[0]

        keys_raw = ring("keys_raw", 6, [P, COLS], BF16)
        values_raw = ring("values_raw", 3, [P, COLS], BF16)
        state_raw = ring("state_raw", 3, [P, COLS], BF16)
        negative = ring("negative", 3, [P, COLS], BF16)
        exp_branch = ring("exp_branch", 3, [P, COLS], BF16)
        linear_branch = ring("linear_branch", 3, [P, COLS], BF16)
        feat = ring("feat", 2, [P, COLS], BF16)
        feat_words = ring("feat_words", 2, [P, COLS], BF16)
        feat_codes = ring("feat_codes", 2, [P, GROUP], U32)
        feat_scales = ring("feat_scales", 2, [P, GROUP], U8)
        values_signed = ring("values_signed", 2, [P, COLS], BF16)
        values_words = ring("values_words", 2, [P, COLS], BF16)
        values_codes = ring("values_codes", 4, [P, DV], U32)
        values_scales = ring("values_scales", 4, [P, DV], U8)
        kept = ring("kept", 4, [P, DV], F32)
        y = ring("y", 3, [P, COLS], F32)
        y_words = ring("y_words", 2, [P, COLS], BF16)
        y_codes = ring("y_codes", 2, [P, DV], U32)
        y_scales = one("y_scales", [P, H * DV], U8)
        upd = [psum.tile([P, DV], F32, name="upd%d" % i) for i in range(2 * PACK)]

        width = VALUE_TILES * PACK
        write_sb = one("write_sb", [P, width], BF16)
        gain_sb = one("gain_sb", [P, width], BF16)
        keep_sb = one("keep_sb", [P, width], BF16)
        keep_f32 = one("keep_f32", [P, width], F32)
        sign_twice = one("sign_twice", [P, width], F32)
        sign = one("sign", [P, width], F32)
        size = one("size", [P, width], F32)
        size_low = one("size_low", [P, width], F32)
        factors = one("factors", [P, 3 * width], F32)
        ln_factors = one("ln_factors", [P, 3 * width], F32)
        ln_size = one("ln_size", [P, width], F32)

        def slot(tile, j):
            return tile[:, j * GROUP : (j + 1) * GROUP]

        def column(tile, index, j):
            return tile[:, index * PACK + j : index * PACK + j + 1]

        def rows_of(tensor, head, group):
            return tensor[head, group * GROUP : (group + 1) * GROUP, :].rearrange("(p j) c -> p j c", j=PACK)

        def by_slot(tile):
            return tile[:].rearrange("p (j c) -> p j c", j=PACK)

        def value_tile(step):
            return step // (CHANNEL_GROUPS * TOKEN_GROUPS) * TOKEN_GROUPS + step % TOKEN_GROUPS

        def load_vector(tile, vector):
            nc.sync.dma_start(
                out=tile[:].rearrange("p (k j) -> p k j", j=PACK),
                in_=vector.rearrange("h (g p j) -> p (h g) j", p=P, j=PACK),
            )

        def load_keys(step):
            head, channel_group = divmod(step // TOKEN_GROUPS, CHANNEL_GROUPS)
            rows = rows_of(keys, head, step % TOKEN_GROUPS)
            nc.sync.dma_start(
                out=by_slot(keys_raw[step % len(keys_raw)]),
                in_=rows[:, :, channel_group * GROUP : (channel_group + 1) * GROUP],
            )

        def load_values(k):
            nc.sync.dma_start(out=by_slot(values_raw[k % len(values_raw)]), in_=rows_of(values, *divmod(k, TOKEN_GROUPS)))

        def load_state(block):
            nc.sync.dma_start(out=by_slot(state_raw[block % len(state_raw)]), in_=rows_of(state, *divmod(block, CHANNEL_GROUPS)))

        def prepare_write():
            nc.vector.scalar_tensor_tensor(size[:], write_sb[:], -1.0, write_sb[:], ALU.mult, ALU.max)
            nc.vector.tensor_scalar(sign_twice[:], write_sb[:], 0.0, 2.0, ALU.is_ge, ALU.mult)
            nc.vector.tensor_scalar(size_low[:], size[:], SMALLEST_NORMAL, LN_LOW, ALU.max, ALU.min)
            nc.vector.tensor_scalar(factors[:, 0:width], size[:], LN_LOW, LN_HIGH, ALU.max, ALU.min)
            nc.vector.tensor_scalar(factors[:, width : 2 * width], size[:], LN_HIGH, LN_LOW, ALU.max, ALU.mult)
            nc.vector.tensor_scalar(factors[:, 2 * width :], size_low[:], LN_HIGH, None, ALU.mult)
            nc.vector.tensor_scalar(sign[:], sign_twice[:], -1.0, None, ALU.add)
            nc.scalar.activation(ln_factors[:], factors[:], ACT.Ln)

        def sum_logs():
            nc.vector.tensor_reduce(
                ln_size[:], ln_factors[:].rearrange("p (r c) -> p c r", r=3), mybir.AxisListType.X, ALU.add
            )

        def negative_part(step):
            nc.vector.tensor_scalar(negative[step % 3][:], keys_raw[step % len(keys_raw)][:], 0.0, None, ALU.min)

        def linear(step):
            for j in range(PACK):
                nc.vector.tensor_scalar(
                    slot(linear_branch[step % 3], j), slot(keys_raw[step % len(keys_raw)], j),
                    1.0, column(size, value_tile(step), j), ALU.add, ALU.mult,
                )

        def exponential(step):
            for j in range(PACK):
                nc.scalar.activation(
                    slot(exp_branch[step % 3], j), slot(negative[step % 3], j), ACT.Exp,
                    bias=column(ln_size, value_tile(step), j),
                )

        def combine(step):
            nc.vector.tensor_tensor(feat[step % 2][:], exp_branch[step % 3][:], linear_branch[step % 3][:], ALU.max)

        def interleave_feat(copy, step, start, stop):
            if start == stop:
                return
            source = feat[step % 2][:].rearrange("p (j m i t) -> p m t j i", j=PACK, i=RUN, t=PACK)
            target = feat_words[step % 2][:].rearrange("p (t m i j) -> p m t j i", j=PACK, i=RUN, t=PACK)
            copy(target[:, start // RUN : stop // RUN], source[:, start // RUN : stop // RUN])

        def interleave(copy, target, source):
            copy(
                target.rearrange("p (c i j) -> p c j i", i=RUN, j=PACK),
                source.rearrange("p j (c i) -> p c j i", i=RUN),
            )

        def quantize(codes, scales, words):
            nc.vector.quantize_mx(out=codes.bitcast(FP8X4), scales=scales, in_=words)

        def column_parts(block):
            if block < BLOCKS - 1:
                return [slice(0, DV)]
            return [slice(0, DV // 2), slice(DV // 2, DV)]

        def sums(block, t, part):
            cols = column_parts(block)[part]
            return upd[(block + part) % 2 * PACK + t][:, 0 : cols.stop - cols.start]

        def multiply(step):
            block, token_group = divmod(step, TOKEN_GROUPS)
            k = value_tile(step) % len(values_codes)
            for part, cols in enumerate(column_parts(block)):
                for t in range(PACK):
                    channels = slice(t * P, (t + 1) * P)
                    nc.tensor.matmul_mx(
                        out=sums(block, t, part),
                        lhsT=feat_codes[step % 2][:, channels].bitcast(FP8X4),
                        lhsT_scale=feat_scales[step % 2][:, channels],
                        rhs=values_codes[k][:, cols].bitcast(FP8X4),
                        rhs_scale=values_scales[k][:, cols],
                        start=token_group == 0,
                        stop=token_group == TOKEN_GROUPS - 1,
                    )

        def quantize_feat(step):
            quantize(feat_codes[step % 2][:], feat_scales[step % 2][:], feat_words[step % 2][:])
            multiply(step)

        def sign_values(k):
            for j in range(PACK):
                nc.vector.tensor_scalar(
                    slot(values_signed[k % 2], j), slot(values_raw[k % len(values_raw)], j),
                    column(sign, k, j), None, ALU.mult,
                )

        def interleave_values(copy, k):
            interleave(copy, values_words[k % 2][:], by_slot(values_signed[k % 2]))

        def quantize_values(k):
            quantize(values_codes[k % len(values_codes)][:], values_scales[k % len(values_scales)][:], values_words[k % 2][:])

        def kept_tile(block, t):
            if block > 0 and t == GPSIMD_SLOTS[0]:
                return linear_branch[2 * block % 3][:].bitcast(F32)[:, 0:DV]
            return kept[t][:]

        def keep_state_scalar(block, t):
            nc.scalar.activation(
                kept_tile(block, t), slot(state_raw[block % len(state_raw)], t), ACT.Copy, scale=column(keep_f32, block, t)
            )

        def keep_state(engine, block, t):
            engine.tensor_scalar(
                kept_tile(block, t), slot(state_raw[block % len(state_raw)], t), column(keep_f32, block, t), 0.0,
                ALU.mult, ALU.add,
            )

        def new_state(block, part):
            cols = column_parts(block)[part]
            for t in range(PACK):
                nc.vector.scalar_tensor_tensor(
                    slot(y[block % len(y)], t)[:, cols], sums(block, t, part), column(gain_sb, block, t),
                    kept_tile(block, t)[:, cols], ALU.mult, ALU.add,
                )
                if t % 2 == 1:
                    nc.sync.dma_start(
                        out=rows_of(out_0, *divmod(block, CHANNEL_GROUPS))[:, t - 1 : t + 1, cols],
                        in_=by_slot(y[block % len(y)])[:, t - 1 : t + 1, cols],
                    )

        def interleave_state(copy, block, start, stop):
            interleave(
                copy, y_words[block % 2][:, PACK * start : PACK * stop], by_slot(y[block % len(y)])[:, :, start:stop]
            )

        def quantize_state(block, start, stop):
            head, channel_group = divmod(block, CHANNEL_GROUPS)
            cols = slice(head * DV + start, head * DV + stop)
            codes = y_codes[block % 2][:, start:stop]
            quantize(codes, y_scales[4 * channel_group :, cols], y_words[block % 2][:, PACK * start : PACK * stop])
            nc.sync.dma_start(
                out=out_1[channel_group, :, cols, :].rearrange("p m t -> p (m t)").bitcast(I32), in_=codes.bitcast(I32)
            )

        def store_scales(head, queues):
            cols = slice(head * DV, (head + 1) * DV)
            for quadrant in range(4):
                queues[quadrant % len(queues)].dma_start(
                    out=out_2[:, 4 * quadrant : 4 * quadrant + 4, cols].bitcast(I32),
                    in_=y_scales[32 * quadrant : 32 * quadrant + 4 * CHANNEL_GROUPS, cols].bitcast(I32),
                )

        load_vector(write_sb, write)
        load_keys(0)
        load_values(0)
        load_keys(1)
        load_keys(2)
        load_values(1)
        load_vector(keep_sb, keep)
        load_state(0)
        load_keys(3)
        load_values(2)
        load_vector(gain_sb, gain)
        load_state(1)
        load_keys(4)

        prepare_write()
        negative_part(0)
        sum_logs()
        linear(0)
        exponential(0)
        sign_values(0)
        negative_part(1)
        exponential(1)
        interleave_values(nc.vector.tensor_copy, 0)

        last = BLOCKS - 1
        for step in range(STEPS):
            pair, odd = divmod(step, 2)
            split = P - scalar_share(step)
            if step + 5 < STEPS:
                load_keys(step + 5)
            if step + 2 < STEPS:
                negative_part(step + 2)
                exponential(step + 2)
            combine(step)
            interleave_feat(nc.scalar.copy, step, split, P)
            if step == 0:
                sign_values(1)
            if odd and pair + 2 < VALUE_TILES:
                sign_values(pair + 2)
                if pair + 3 < VALUE_TILES:
                    load_values(pair + 3)
            if not odd and pair >= 1:
                new_state(pair - 1, 0)
                for t in GPSIMD_SLOTS:
                    keep_state(nc.gpsimd, pair, t)
            if odd and pair >= 1:
                for t in VECTOR_SLOTS:
                    keep_state(nc.vector, pair, t)
            if odd and pair >= 2:
                quantize_state(pair - 2, 0, DV)
                if pair % 2 == 1:
                    store_scales(pair // 2 - 1, [nc.sync])
            interleave_feat(nc.vector.tensor_copy, step, 0, split)
            if step + 1 < STEPS:
                linear(step + 1)
            if step == 0:
                quantize_values(0)
                nc.vector.tensor_copy(keep_f32[:], keep_sb[:])
            if odd and pair + 1 < VALUE_TILES:
                quantize_values(pair + 1)
            quantize_feat(step)
            if not odd and pair < last:
                interleave_values(nc.scalar.copy, pair + 1)
            if not odd and pair == last:
                interleave_state(nc.scalar.copy, last - 1, 0, DV)
            if odd:
                for t in range(PACK):
                    if t not in GPSIMD_SLOTS + VECTOR_SLOTS or pair == 0:
                        keep_state_scalar(pair, t)
                if pair + 2 < BLOCKS:
                    load_state(pair + 2)
            if odd and 1 <= pair < last:
                interleave_state(nc.scalar.copy, pair - 1, 0, DV)

        half = DV // 2
        quantize_state(last - 1, 0, DV)
        new_state(last, 0)
        new_state(last, 1)
        interleave_state(nc.scalar.copy, last, 0, half)
        interleave_state(nc.scalar.copy, last, half + TAIL_SPLIT, DV)
        quantize_state(last, 0, half)
        interleave_state(nc.vector.tensor_copy, last, half, half + TAIL_SPLIT)
        quantize_state(last, half, DV)
        store_scales(H - 1, [nc.scalar, nc.sync])
